import numpy as np
import ml_dtypes


def mxq(x, axis, fmt="e4m3"):
    dtype, down = {"e4m3": (ml_dtypes.float8_e4m3fn, 7), "e5m2": (ml_dtypes.float8_e5m2, 14)}[fmt]
    v = np.moveaxis(np.asarray(x, np.float32).astype(ml_dtypes.bfloat16).astype(np.float64), axis, -1)
    blocks = v.reshape(v.shape[:-1] + (-1, 32))
    amax = np.abs(blocks).max(-1, keepdims=True)
    byte = np.maximum(np.where(amax > 0, np.frexp(amax)[1] - 1 + 127, 0) - down, 1)
    scale = np.exp2(byte - 127.0)
    codes = (blocks / scale).astype(np.float32).astype(dtype).astype(np.float64)
    return np.moveaxis((codes * scale).reshape(v.shape), -1, axis)


WIDE = False


def mx_kscale(k):
    if not WIDE:
        return np.ones(k)
    levels = np.array([10, -10, 5, -5, 0])
    if k % 512:
        return np.exp2(np.random.permutation(np.resize(levels, k // 32))).repeat(32)
    a = np.empty((k // 512, 16))
    for p in range(k // 512):
        a[p, :8] = np.random.permutation(np.resize(levels, 8))
        for g in range(8):
            far = levels[np.abs(levels - a[p, g]) >= 10]
            a[p, g + 8] = far[np.random.randint(len(far))]
    return np.exp2(a.ravel()).repeat(32)


def f64(x):
    return np.asarray(x).astype(np.float64)


def striped(idx):
    return np.tile(np.asarray(idx).reshape(-1, 16).T, (8, 1)).astype(np.uint16)


def unstriped(offs):
    return offs[:16].T.reshape(-1).astype(np.int64)


E2M1 = np.array([0.0, 0.5, 1.0, 1.5, 2.0, 3.0, 4.0, 6.0, -0.0, -0.5, -1.0, -1.5, -2.0, -3.0, -4.0, -6.0])


def pack_weight(w, fmt):
    k, n = w.shape
    w = f64(np.asarray(w, np.float32).astype(ml_dtypes.bfloat16)).reshape(k // 32, 32, n)
    amax = np.abs(w).max(1)
    if fmt == "e4m3":
        byte = np.frexp(amax)[1] - 1 + 127 - 7
    else:
        mant, ex = np.frexp(amax / 6.0)
        byte = np.where(mant > 0.5, ex, ex - 1) + 127
    byte = np.clip(np.where(amax > 0, byte, 1), 1, 254)
    scaled = (w * np.exp2(127.0 - byte)[:, None, :]).reshape(k, n).astype(np.float32)
    by_word = np.ascontiguousarray(scaled.reshape(k // 512, 128, 4, n).transpose(0, 1, 3, 2))
    if fmt == "e4m3":
        words = by_word.astype(ml_dtypes.float8_e4m3fn).view(np.uint8)
    else:
        c = by_word.astype(ml_dtypes.float4_e2m1fn).view(np.uint8) & 0xF
        words = (c[..., 0::2] | (c[..., 1::2] << 4)).reshape(k // 512, 128, 2 * n)
    return np.ascontiguousarray(words), np.ascontiguousarray(byte.astype(np.uint8).reshape(k // 512, 16, n))


def unpack_weight(words, scales, fmt):
    g, _, n = scales.shape
    words = np.ascontiguousarray(words).reshape(g, 128, n, -1)
    if fmt == "e4m3":
        vals = words.view(ml_dtypes.float8_e4m3fn).astype(np.float64)
    else:
        nib = np.empty((g, 128, n, 4), np.uint8)
        nib[..., 0::2] = words & 0xF
        nib[..., 1::2] = words >> 4
        vals = E2M1[nib]
    vals = vals * np.repeat(np.exp2(scales.astype(np.float64) - 127.0), 8, axis=1)[..., None]
    return vals.transpose(0, 1, 3, 2).reshape(g * 512, n)


K, R, F, T, J, G = 512, 128, 512, 2048, 512, 64


def setup_inputs():
    n = np.random.standard_normal
    idx = np.random.permutation(T)[:J]
    fk = mx_kscale(K)
    ff = mx_kscale(F)
    tabp = pack_weight(n((K, T)) / fk[:, None], "e2m1")
    return {
        "tab_words": tabp[0],
        "tab_scales": tabp[1],
        "w1": (n((K, R)) * 1.5 / np.sqrt(K) * fk[:, None]).astype(np.float32),
        "w2": (n((K, R)) * 0.7 / np.sqrt(K) * fk[:, None]).astype(np.float32),
        "wo": (n((F, R)) * 1 / np.sqrt(F) * ff[:, None]).astype(np.float32),
        "dy": (n((F, G)) / ff[:, None]).astype(np.float32),
        "og": (np.random.uniform(0.3, 1.0, (R, 1))).astype(np.float32),
        "base": (0.3 * n((R, J))).astype(np.float32),
        "offs": striped(idx),
    }


def reference(tab_words, tab_scales, w1, w2, wo, dy, og, base, offs):
    idx = unstriped(offs)
    tabu = unpack_weight(tab_words, tab_scales, "e2m1")
    w1q = mxq(f64(w1), 0, "e4m3")
    tabidxg = tabu[:, idx]
    a = w1q.T @ tabidxg
    w2q = mxq(f64(w2), 0, "e4m3")
    b = w2q.T @ tabidxg
    p = np.exp(b)
    z = p.reshape(R, G, J // G).sum(axis=2)
    n1 = (p * a).reshape(R, G, J // G).sum(axis=2)
    u1 = np.tanh(n1 / z)
    woq = mxq(f64(wo), 0, "e4m3")
    dyq = mxq(f64(dy), 0, "e4m3")
    c0 = woq.T @ dyq
    dn1 = c0 * (1.0 - np.square(u1)) / z
    r1 = np.repeat(dn1, J // G, axis=1)
    dz = c0 * (1.0 - np.square(u1)) * n1 / np.square(z) * (-1.0)
    r2 = np.repeat(dz, J // G, axis=1)
    dp = r1 * a + r2
    db = dp * p
    hdb = db * 2.0
    hdp = hdb * p
    hdz = hdp.reshape(R, G, J // G).sum(axis=2)
    hr1 = hdp * a
    hdn1 = hr1.reshape(R, G, J // G).sum(axis=2)
    hu1 = hdz * (-1.0) / np.square(z) * n1 * c0 * (-1.0) * u1 * 2.0 + hdn1 / z * c0 * (-1.0) * u1 * 2.0
    hn1 = hdz * (-1.0) / np.square(z) * c0 * (1.0 - np.square(u1)) + hu1 * (1.0 - np.square(u1)) / z
    r51 = np.repeat(hn1, J // G, axis=1)
    hz = hdz * (-1.0) * c0 * (1.0 - np.square(u1)) * n1 / np.square(np.square(z)) * (-1.0) * z * 2.0 - hdn1 * c0 * (1.0 - np.square(u1)) / np.square(z) - hu1 * (1.0 - np.square(u1)) * n1 / np.square(z)
    r52 = np.repeat(hz, J // G, axis=1)
    hp = hdb * dp + r51 * a + r52
    hb = hp * p
    y = hb * f64(og) + f64(base)
    return y

@@ -1,0 +1,158 @@
+from contextlib import ExitStack
+
+import concourse.mybir as mybir
+
+K, R, F, T, J, G = 512, 128, 512, 2048, 512, 64
+FLOPS = 2 * K * R * J * 2 + 2 * F * R * G
+
+F32 = mybir.dt.float32
+BF16 = mybir.dt.bfloat16
+I32 = mybir.dt.int32
+U32 = mybir.dt.uint32
+U16 = mybir.dt.uint16
+U8 = mybir.dt.uint8
+FP8X4 = mybir.dt.float8_e4m3fn_x4
+FP4X4 = mybir.dt.float4_e2m1fn_x4
+ACT = mybir.ActivationFunctionType
+ALU = mybir.AluOpType
+AX = mybir.AxisListType
+
+P = 128
+PACK = 4
+POOL = J // G
+HALVES = 2
+JH = J // HALVES
+GH = G // HALVES
+
+
+def tile_attend_gpgatepool_kernel(tc, tab_words, tab_scales, w1, w2, wo, dy, og, base, offs, out):
+    nc = tc.nc
+    with ExitStack() as ctx:
+        sb = ctx.enter_context(tc.tile_pool(name="sb", bufs=1))
+        ps = ctx.enter_context(tc.psum_pool(name="ps", bufs=1))
+        V = nc.vector
+        both = range(HALVES)
+
+        def spread(x):
+            return x.rearrange("p (g o) -> p g o", o=1).to_broadcast([P, x.shape[1], POOL])
+
+        def grouped(x):
+            return x.rearrange("p (g i) -> p g i", i=POOL)
+
+        def by_rows(rows):
+            return rows.rearrange("(p t) c -> p t c", t=PACK)
+
+        offsets = sb.tile([P, J // 16], U16, name="offsets")
+        nc.sync.dma_start(offsets[:], offs)
+        scales = sb.tile([P, T], U8, name="scales")
+        V.memset(scales[:].bitcast(I32), 0)
+        for q in range(4):
+            nc.scalar.dma_start(out=scales[32 * q : 32 * q + 4, :].bitcast(I32), in_=tab_scales[0, 4 * q : 4 * q + 4, :].bitcast(I32))
+        w2_raw = sb.tile([P, PACK, R], F32, name="w2_raw", tag="stage_a")
+        nc.sync.dma_start(out=w2_raw[:], in_=by_rows(w2))
+        words = sb.tile([P, T], U16, name="words")
+        nc.sync.dma_start(out=words[:].bitcast(I32), in_=tab_words[0].bitcast(I32))
+        w1_raw = sb.tile([P, PACK, R], F32, name="w1_raw", tag="stage_b")
+        nc.sync.dma_start(out=w1_raw[:], in_=by_rows(w1))
+
+        def weave(name, raw):
+            woven = sb.tile([P, raw.shape[2], PACK], BF16, name=name + "_woven", align_bytes=64)
+            nc.scalar.copy(out=woven[:], in_=raw.rearrange("p t c -> p c t"))
+            return woven
+
+        def quantize(name, woven):
+            width = woven.shape[1]
+            codes = sb.tile([P, width], U32, name=name + "_codes", align_bytes=64)
+            plane = sb.tile([P, width], U8, name=name + "_plane", align_bytes=64)
+            V.quantize_mx(out=codes[:].bitcast(FP8X4), scales=plane[:], in_=woven[:].rearrange("p c t -> p (c t)"))
+            return codes, plane
+
+        def product(name, weights, moving, moving_scales):
+            acc = ps.tile([P, moving.shape[1]], F32, name=name)
+            nc.tensor.matmul_mx(out=acc[:], lhsT=weights[0][:].bitcast(FP8X4), lhsT_scale=weights[1][:],
+                                rhs=moving, rhs_scale=moving_scales, start=True, stop=True)
+            return acc
+
+        def gather(name, dtype, window, h):
+            picked = sb.tile([P, JH], dtype, name=f"{name}{h}", align_bytes=64)
+            V.tensor_copy(picked[:], window[:].indirect(offsets[:, h * JH // 16 : (h + 1) * JH // 16]))
+            return picked
+
+        col_scales = [gather("col_scales", U8, scales, h) for h in both]
+        w2_q = quantize("w2", weave("w2", w2_raw[:]))
+        col_words = [gather("col_words", U16, words, h) for h in both]
+        b = [product(f"b{h}", w2_q, col_words[h][:].bitcast(FP4X4), col_scales[h][:]) for h in both]
+        w1_q = quantize("w1", weave("w1", w1_raw[:]))
+        a = [product(f"a{h}", w1_q, col_words[h][:].bitcast(FP4X4), col_scales[h][:]) for h in both]
+
+        last_raw = sb.tile([P, PACK * (R + G)], F32, name="last_raw", tag="stage_a")
+        wo_raw = last_raw[:, 0 : PACK * R].rearrange("p (t c) -> p t c", t=PACK)
+        dy_raw = last_raw[:, PACK * R :].rearrange("p (t c) -> p t c", t=PACK)
+        nc.sync.dma_start(out=wo_raw, in_=by_rows(wo))
+        nc.sync.dma_start(out=dy_raw, in_=by_rows(dy))
+        tail_in = sb.tile([P, J + 8], F32, name="tail_in", tag="stage_b")
+        base_sb = tail_in[:, 0:J]
+        gain = tail_in[:, J : J + 1]
+        nc.sync.dma_start(out=base_sb, in_=base)
+        nc.sync.dma_start(out=gain, in_=og)
+
+        def new(name, width):
+            return [sb.tile([P, width], F32, name=f"{name}{h}") for h in both]
+
+        p, pa, d, e, kp, t1, t2, t3, t4, y = [new(n, JH) for n in ("p", "pa", "d", "e", "kp", "t1", "t2", "t3", "t4", "y")]
+        z, n1, rz, m, u, uu, nq, slope, kk, ub, cc = [new(n, GH) for n in ("z", "n1", "rz", "m", "u", "uu", "nq", "slope", "kk", "ub", "cc")]
+        bwd = new("bwd", 2 * JH)
+        ab = new("ab", 2 * GH)
+        abz = new("abz", 2 * GH)
+
+        for h in both:
+            nc.scalar.activation(out=p[h][:], in_=b[h][:], func=ACT.Exp)
+        wo_q = quantize("wo", weave("wo", wo_raw))
+        dy_q = quantize("dy", weave("dy", dy_raw))
+        c0 = product("c0", wo_q, dy_q[0][:].bitcast(FP8X4), dy_q[1][:])
+        gain2 = sb.tile([P, 1], F32, name="gain2")
+        nc.scalar.activation(out=gain2[:], in_=gain, func=ACT.Copy, scale=2.0)
+
+        for h in both:
+            V.tensor_reduce(out=z[h][:], in_=grouped(p[h][:]), axis=AX.X, op=ALU.add)
+            V.tensor_tensor(pa[h][:], a[h][:], p[h][:], ALU.mult)
+            V.reciprocal(rz[h][:], z[h][:])
+            V.tensor_reduce(out=n1[h][:], in_=grouped(pa[h][:]), axis=AX.X, op=ALU.add)
+        for h in both:
+            V.tensor_tensor(m[h][:], n1[h][:], rz[h][:], ALU.mult)
+            nc.scalar.activation(out=u[h][:], in_=m[h][:], func=ACT.Tanh)
+            nc.scalar.activation(out=uu[h][:], in_=u[h][:], func=ACT.Square)
+        for h in both:
+            V.tensor_tensor(grouped(d[h][:]), grouped(a[h][:]), spread(m[h][:]), ALU.subtract)
+        for h in both:
+            V.tensor_tensor(e[h][:], d[h][:], p[h][:], ALU.mult)
+        for h in both:
+            nc.scalar.activation(out=bwd[h][:, JH:], in_=e[h][:], func=ACT.Square)
+            V.tensor_tensor(bwd[h][:, 0:JH], e[h][:], p[h][:], ALU.mult)
+        for h in both:
+            V.scalar_tensor_tensor(nq[h][:], uu[h][:], 1.0, c0[:, h * GH : (h + 1) * GH], ALU.subtract, ALU.mult)
+        for h in both:
+            V.tensor_tensor(slope[h][:], nq[h][:], rz[h][:], ALU.mult)
+            nc.scalar.activation(out=kk[h][:], in_=slope[h][:], func=ACT.Square)
+        for h in both:
+            V.tensor_reduce(out=ab[h][:], in_=grouped(bwd[h][:]), axis=AX.X, op=ALU.add)
+        for h in both:
+            V.tensor_tensor(abz[h][:].rearrange("p (s g) -> p s g", s=2), ab[h][:].rearrange("p (s g) -> p s g", s=2),
+                            rz[h][:].rearrange("p (o g) -> p o g", o=1).to_broadcast([P, 2, GH]), ALU.mult)
+        for h in both:
+            V.scalar_tensor_tensor(ub[h][:], abz[h][:, GH:], 2.0, u[h][:], ALU.mult, ALU.mult)
+        for h in both:
+            V.tensor_tensor(grouped(kp[h][:]), grouped(p[h][:]), spread(kk[h][:]), ALU.mult)
+        for h in both:
+            V.tensor_tensor(cc[h][:], abz[h][:, 0:GH], ub[h][:], ALU.add)
+        for h in both:
+            V.tensor_tensor(grouped(t1[h][:]), grouped(e[h][:]), spread(cc[h][:]), ALU.subtract)
+        for h in both:
+            V.tensor_tensor(t2[h][:], t1[h][:], d[h][:], ALU.mult)
+        for h in both:
+            V.tensor_tensor(grouped(t3[h][:]), grouped(t2[h][:]), spread(abz[h][:, GH:]), ALU.subtract)
+        for h in both:
+            V.tensor_tensor(t4[h][:], t3[h][:], kp[h][:], ALU.mult)
+        for h in both:
+            V.scalar_tensor_tensor(y[h][:], t4[h][:], gain2[:], base_sb[:, h * JH : (h + 1) * JH], ALU.mult, ALU.add)
+            nc.sync.dma_start(out=out[:, h * JH : (h + 1) * JH], in_=y[h][:])

@@ -1,3 +1,4 @@
+import math
 from contextlib import ExitStack
 
 import concourse.mybir as mybir
@@ -44,20 +45,20 @@ def tile_attend_gpgatepool_kernel(tc, tab_words, tab_scales, w1, w2, wo, dy, og,
 
         offsets = sb.tile([P, J // 16], U16, name="offsets")
         nc.sync.dma_start(offsets[:], offs)
+        words = sb.tile([P, T], U16, name="words")
+        nc.sync.dma_start(out=words[:].bitcast(I32), in_=tab_words[0].bitcast(I32))
         scales = sb.tile([P, T], U8, name="scales")
         V.memset(scales[:].bitcast(I32), 0)
         for q in range(4):
-            nc.scalar.dma_start(out=scales[32 * q : 32 * q + 4, :].bitcast(I32), in_=tab_scales[0, 4 * q : 4 * q + 4, :].bitcast(I32))
-        w2_raw = sb.tile([P, PACK, R], F32, name="w2_raw", tag="stage_a")
+            nc.sync.dma_start(out=scales[32 * q : 32 * q + 4, :].bitcast(I32), in_=tab_scales[0, 4 * q : 4 * q + 4, :].bitcast(I32))
+        w2_raw = sb.tile([P, PACK, R], F32, name="w2_raw")
         nc.sync.dma_start(out=w2_raw[:], in_=by_rows(w2))
-        words = sb.tile([P, T], U16, name="words")
-        nc.sync.dma_start(out=words[:].bitcast(I32), in_=tab_words[0].bitcast(I32))
-        w1_raw = sb.tile([P, PACK, R], F32, name="w1_raw", tag="stage_b")
+        w1_raw = sb.tile([P, PACK, R], F32, name="w1_raw", tag="stage_b", align_bytes=64)
         nc.sync.dma_start(out=w1_raw[:], in_=by_rows(w1))
 
         def weave(name, raw):
             woven = sb.tile([P, raw.shape[2], PACK], BF16, name=name + "_woven", align_bytes=64)
-            nc.scalar.copy(out=woven[:], in_=raw.rearrange("p t c -> p c t"))
+            nc.scalar.copy(out=woven[:].rearrange("p (c i) t -> p c t i", i=4), in_=raw.rearrange("p t (c i) -> p c t i", i=4))
             return woven
 
         def quantize(name, woven):
@@ -73,24 +74,26 @@ def tile_attend_gpgatepool_kernel(tc, tab_words, tab_scales, w1, w2, wo, dy, og,
                                 rhs=moving, rhs_scale=moving_scales, start=True, stop=True)
             return acc
 
-        def gather(name, dtype, window, h):
-            picked = sb.tile([P, JH], dtype, name=f"{name}{h}", align_bytes=64)
+        def gather(picked, window, h):
             V.tensor_copy(picked[:], window[:].indirect(offsets[:, h * JH // 16 : (h + 1) * JH // 16]))
             return picked
 
-        col_scales = [gather("col_scales", U8, scales, h) for h in both]
+        col_words = [gather(sb.tile([P, JH], U16, name=f"col_words{h}", align_bytes=64), words, h) for h in both]
+        col_scales = [gather(sb.tile([P, JH], U8, name="col_scales0", align_bytes=64), scales, 0)]
         w2_q = quantize("w2", weave("w2", w2_raw[:]))
-        col_words = [gather("col_words", U16, words, h) for h in both]
-        b = [product(f"b{h}", w2_q, col_words[h][:].bitcast(FP4X4), col_scales[h][:]) for h in both]
         w1_q = quantize("w1", weave("w1", w1_raw[:]))
-        a = [product(f"a{h}", w1_q, col_words[h][:].bitcast(FP4X4), col_scales[h][:]) for h in both]
+        col_scales.append(gather(sb.tile([P, JH], U8, name="col_scales1", tag="stage_b", align_bytes=64), scales, 1))
+        a, b = [], []
+        for h in both:
+            b.append(product(f"b{h}", w2_q, col_words[h][:].bitcast(FP4X4), col_scales[h][:]))
+            a.append(product(f"a{h}", w1_q, col_words[h][:].bitcast(FP4X4), col_scales[h][:]))
 
-        last_raw = sb.tile([P, PACK * (R + G)], F32, name="last_raw", tag="stage_a")
+        last_raw = sb.tile([P, PACK * (R + G)], F32, name="last_raw")
         wo_raw = last_raw[:, 0 : PACK * R].rearrange("p (t c) -> p t c", t=PACK)
         dy_raw = last_raw[:, PACK * R :].rearrange("p (t c) -> p t c", t=PACK)
         nc.sync.dma_start(out=wo_raw, in_=by_rows(wo))
         nc.sync.dma_start(out=dy_raw, in_=by_rows(dy))
-        tail_in = sb.tile([P, J + 8], F32, name="tail_in", tag="stage_b")
+        tail_in = sb.tile([P, J + 8], F32, name="tail_in")
         base_sb = tail_in[:, 0:J]
         gain = tail_in[:, J : J + 1]
         nc.sync.dma_start(out=base_sb, in_=base)
@@ -99,60 +102,140 @@ def tile_attend_gpgatepool_kernel(tc, tab_words, tab_scales, w1, w2, wo, dy, og,
         def new(name, width):
             return [sb.tile([P, width], F32, name=f"{name}{h}") for h in both]
 
-        p, pa, d, e, kp, t1, t2, t3, t4, y = [new(n, JH) for n in ("p", "pa", "d", "e", "kp", "t1", "t2", "t3", "t4", "y")]
-        z, n1, rz, m, u, uu, nq, slope, kk, ub, cc = [new(n, GH) for n in ("z", "n1", "rz", "m", "u", "uu", "nq", "slope", "kk", "ub", "cc")]
-        bwd = new("bwd", 2 * JH)
-        ab = new("ab", 2 * GH)
-        abz = new("abz", 2 * GH)
+        p, pa, d, e, ee, pe, kp, t1, t2, t3, t4, y = [new(n, JH) for n in ("p", "pa", "d", "e", "ee", "pe", "kp", "t1", "t2", "t3", "t4", "y")]
+        z, n1, m, u, ub, sa = [new(n, GH) for n in ("z", "n1", "m", "u", "ub", "sa")]
+        cb = new("cb", 2 * GH)
+        cbz = new("cbz", 2 * GH)
+        rz_all, uu, nq, slope, kk = [sb.tile([P, G], F32, name=n) for n in ("rz_all", "uu", "nq", "slope", "kk")]
+        rz = [rz_all[:, h * GH : (h + 1) * GH] for h in both]
 
+        wo_woven = weave("wo", wo_raw)
         for h in both:
             nc.scalar.activation(out=p[h][:], in_=b[h][:], func=ACT.Exp)
-        wo_q = quantize("wo", weave("wo", wo_raw))
-        dy_q = quantize("dy", weave("dy", dy_raw))
-        c0 = product("c0", wo_q, dy_q[0][:].bitcast(FP8X4), dy_q[1][:])
-        gain2 = sb.tile([P, 1], F32, name="gain2")
-        nc.scalar.activation(out=gain2[:], in_=gain, func=ACT.Copy, scale=2.0)
+        dy_woven = weave("dy", dy_raw)
+        last_q = {}
+        c0 = ps.tile([P, G], F32, name="c0")
 
-        for h in both:
+        def s_z(h):
             V.tensor_reduce(out=z[h][:], in_=grouped(p[h][:]), axis=AX.X, op=ALU.add)
+
+        def s_pa(h):
             V.tensor_tensor(pa[h][:], a[h][:], p[h][:], ALU.mult)
-            V.reciprocal(rz[h][:], z[h][:])
+
+        def s_rz(h):
+            V.reciprocal(rz[h], z[h][:])
+
+        def s_n(h):
             V.tensor_reduce(out=n1[h][:], in_=grouped(pa[h][:]), axis=AX.X, op=ALU.add)
-        for h in both:
-            V.tensor_tensor(m[h][:], n1[h][:], rz[h][:], ALU.mult)
+
+        def s_m(h):
+            V.tensor_tensor(m[h][:], n1[h][:], rz[h], ALU.mult)
             nc.scalar.activation(out=u[h][:], in_=m[h][:], func=ACT.Tanh)
-            nc.scalar.activation(out=uu[h][:], in_=u[h][:], func=ACT.Square)
-        for h in both:
+            nc.scalar.activation(out=uu[:, h * GH : (h + 1) * GH], in_=u[h][:], func=ACT.Square)
+
+        def s_d(h):
             V.tensor_tensor(grouped(d[h][:]), grouped(a[h][:]), spread(m[h][:]), ALU.subtract)
-        for h in both:
+
+        def s_e(h):
             V.tensor_tensor(e[h][:], d[h][:], p[h][:], ALU.mult)
-        for h in both:
-            nc.scalar.activation(out=bwd[h][:, JH:], in_=e[h][:], func=ACT.Square)
-            V.tensor_tensor(bwd[h][:, 0:JH], e[h][:], p[h][:], ALU.mult)
-        for h in both:
-            V.scalar_tensor_tensor(nq[h][:], uu[h][:], 1.0, c0[:, h * GH : (h + 1) * GH], ALU.subtract, ALU.mult)
-        for h in both:
-            V.tensor_tensor(slope[h][:], nq[h][:], rz[h][:], ALU.mult)
-            nc.scalar.activation(out=kk[h][:], in_=slope[h][:], func=ACT.Square)
-        for h in both:
-            V.tensor_reduce(out=ab[h][:], in_=grouped(bwd[h][:]), axis=AX.X, op=ALU.add)
-        for h in both:
-            V.tensor_tensor(abz[h][:].rearrange("p (s g) -> p s g", s=2), ab[h][:].rearrange("p (s g) -> p s g", s=2),
-                            rz[h][:].rearrange("p (o g) -> p o g", o=1).to_broadcast([P, 2, GH]), ALU.mult)
-        for h in both:
-            V.scalar_tensor_tensor(ub[h][:], abz[h][:, GH:], 2.0, u[h][:], ALU.mult, ALU.mult)
-        for h in both:
-            V.tensor_tensor(grouped(kp[h][:]), grouped(p[h][:]), spread(kk[h][:]), ALU.mult)
-        for h in both:
-            V.tensor_tensor(cc[h][:], abz[h][:, 0:GH], ub[h][:], ALU.add)
-        for h in both:
-            V.tensor_tensor(grouped(t1[h][:]), grouped(e[h][:]), spread(cc[h][:]), ALU.subtract)
-        for h in both:
+            nc.scalar.activation(out=ee[h][:], in_=e[h][:], func=ACT.Square)
+
+        def s_g(h):
+            V.tensor_tensor(pe[h][:], e[h][:], p[h][:], ALU.mult)
+
+        def s_wo(h):
+            last_q["wo"] = quantize("wo", wo_woven)
+
+        def s_dy(h):
+            wo_q = last_q["wo"]
+            dy_q = quantize("dy", dy_woven)
+            nc.tensor.matmul_mx(out=c0[:], lhsT=wo_q[0][:].bitcast(FP8X4), lhsT_scale=wo_q[1][:],
+                                rhs=dy_q[0][:].bitcast(FP8X4), rhs_scale=dy_q[1][:], start=True, stop=True)
+
+        def s_nq(h):
+            V.scalar_tensor_tensor(nq[:], uu[:], 1.0, c0[:], ALU.subtract, ALU.mult)
+
+        def s_slope(h):
+            V.tensor_tensor(slope[:], nq[:], rz_all[:], ALU.mult)
+            nc.scalar.activation(out=kk[:], in_=slope[:], func=ACT.Square, scale=math.sqrt(2.0))
+
+        def s_rf(h):
+            V.tensor_reduce(out=cb[h][:, GH:], in_=grouped(ee[h][:]), axis=AX.X, op=ALU.add)
+
+        def s_rg(h):
+            V.tensor_reduce(out=sa[h][:], in_=grouped(pe[h][:]), axis=AX.X, op=ALU.add)
+
+        def s_ub(h):
+            V.scalar_tensor_tensor(ub[h][:], cb[h][:, GH:], 2.0, u[h][:], ALU.mult, ALU.mult)
+
+        def s_cc(h):
+            V.tensor_tensor(cb[h][:, 0:GH], sa[h][:], ub[h][:], ALU.add)
+
+        def s_x(h):
+            V.tensor_tensor(cbz[h][:].rearrange("p (s g) -> p s g", s=2), cb[h][:].rearrange("p (s g) -> p s g", s=2),
+                            rz[h].rearrange("p (o g) -> p o g", o=1).to_broadcast([P, 2, GH]), ALU.mult)
+
+        def s_kp(h):
+            V.tensor_tensor(grouped(kp[h][:]), grouped(p[h][:]), spread(kk[:, h * GH : (h + 1) * GH]), ALU.mult)
+
+        def s_t1(h):
+            V.tensor_tensor(grouped(t1[h][:]), grouped(e[h][:]), spread(cbz[h][:, 0:GH]), ALU.subtract)
+
+        def s_t2(h):
             V.tensor_tensor(t2[h][:], t1[h][:], d[h][:], ALU.mult)
-        for h in both:
-            V.tensor_tensor(grouped(t3[h][:]), grouped(t2[h][:]), spread(abz[h][:, GH:]), ALU.subtract)
-        for h in both:
+
+        def s_t3(h):
+            V.tensor_tensor(grouped(t3[h][:]), grouped(t2[h][:]), spread(cbz[h][:, GH:]), ALU.subtract)
+
+        def s_t4(h):
             V.tensor_tensor(t4[h][:], t3[h][:], kp[h][:], ALU.mult)
-        for h in both:
-            V.scalar_tensor_tensor(y[h][:], t4[h][:], gain2[:], base_sb[:, h * JH : (h + 1) * JH], ALU.mult, ALU.add)
-            nc.sync.dma_start(out=out[:, h * JH : (h + 1) * JH], in_=y[h][:])
+
+        def s_y(h):
+            pieces = [(0, JH)] if h == 0 else [(0, JH // 2), (JH // 2, JH)]
+            for i, (lo, hi) in enumerate(pieces):
+                V.scalar_tensor_tensor(y[h][:, lo:hi], t4[h][:, lo:hi], gain, base_sb[:, h * JH + lo : h * JH + hi], ALU.mult, ALU.add)
+                queue = nc.scalar if len(pieces) - i == 2 else nc.sync
+                queue.dma_start(out=out[:, h * JH + lo : h * JH + hi], in_=y[h][:, lo:hi])
+
+        s_wo(0)
+        s_z(0)
+        s_pa(0)
+        s_rz(0)
+        s_n(0)
+        s_z(1)
+        s_m(0)
+        s_pa(1)
+        s_rz(1)
+        s_d(0)
+        s_n(1)
+        s_e(0)
+        s_m(1)
+        s_dy(0)
+        s_g(0)
+        s_d(1)
+        s_rg(0)
+        s_e(1)
+        s_rf(0)
+        s_nq(0)
+        s_g(1)
+        s_slope(0)
+        s_ub(0)
+        s_rf(1)
+        s_cc(0)
+        s_rg(1)
+        s_x(0)
+        s_ub(1)
+        s_kp(0)
+        s_cc(1)
+        s_t1(0)
+        s_x(1)
+        s_kp(1)
+        s_t1(1)
+        s_t2(0)
+        s_t2(1)
+        s_t3(0)
+        s_t3(1)
+        s_t4(0)
+        s_t4(1)
+        s_y(0)
+        s_y(1)

import math
from contextlib import ExitStack

import concourse.mybir as mybir

K, R, F, T, J, G = 512, 128, 512, 2048, 512, 64
FLOPS = 2 * K * R * J * 2 + 2 * F * R * G

F32 = mybir.dt.float32
BF16 = mybir.dt.bfloat16
I32 = mybir.dt.int32
U32 = mybir.dt.uint32
U16 = mybir.dt.uint16
U8 = mybir.dt.uint8
FP8X4 = mybir.dt.float8_e4m3fn_x4
FP4X4 = mybir.dt.float4_e2m1fn_x4
ACT = mybir.ActivationFunctionType
ALU = mybir.AluOpType
AX = mybir.AxisListType

P = 128
PACK = 4
POOL = J // G
HALVES = 2
JH = J // HALVES
GH = G // HALVES


def tile_attend_gpgatepool_kernel(tc, tab_words, tab_scales, w1, w2, wo, dy, og, base, offs, out):
    nc = tc.nc
    with ExitStack() as ctx:
        sb = ctx.enter_context(tc.tile_pool(name="sb", bufs=1))
        ps = ctx.enter_context(tc.psum_pool(name="ps", bufs=1))
        V = nc.vector
        both = range(HALVES)

        def spread(x):
            return x.rearrange("p (g o) -> p g o", o=1).to_broadcast([P, x.shape[1], POOL])

        def grouped(x):
            return x.rearrange("p (g i) -> p g i", i=POOL)

        def by_rows(rows):
            return rows.rearrange("(p t) c -> p t c", t=PACK)

        offsets = sb.tile([P, J // 16], U16, name="offsets")
        nc.sync.dma_start(offsets[:], offs)
        words = sb.tile([P, T], U16, name="words")
        nc.sync.dma_start(out=words[:].bitcast(I32), in_=tab_words[0].bitcast(I32))
        scales = sb.tile([P, T], U8, name="scales")
        V.memset(scales[:].bitcast(I32), 0)
        for q in range(4):
            nc.sync.dma_start(out=scales[32 * q : 32 * q + 4, :].bitcast(I32), in_=tab_scales[0, 4 * q : 4 * q + 4, :].bitcast(I32))
        w2_raw = sb.tile([P, PACK, R], F32, name="w2_raw")
        nc.sync.dma_start(out=w2_raw[:], in_=by_rows(w2))
        w1_raw = sb.tile([P, PACK, R], F32, name="w1_raw", tag="stage_b", align_bytes=64)
        nc.sync.dma_start(out=w1_raw[:], in_=by_rows(w1))

        def weave(name, raw):
            woven = sb.tile([P, raw.shape[2], PACK], BF16, name=name + "_woven", align_bytes=64)
            nc.scalar.copy(out=woven[:].rearrange("p (c i) t -> p c t i", i=4), in_=raw.rearrange("p t (c i) -> p c t i", i=4))
            return woven

        def quantize(name, woven):
            width = woven.shape[1]
            codes = sb.tile([P, width], U32, name=name + "_codes", align_bytes=64)
            plane = sb.tile([P, width], U8, name=name + "_plane", align_bytes=64)
            V.quantize_mx(out=codes[:].bitcast(FP8X4), scales=plane[:], in_=woven[:].rearrange("p c t -> p (c t)"))
            return codes, plane

        def product(name, weights, moving, moving_scales):
            acc = ps.tile([P, moving.shape[1]], F32, name=name)
            nc.tensor.matmul_mx(out=acc[:], lhsT=weights[0][:].bitcast(FP8X4), lhsT_scale=weights[1][:],
                                rhs=moving, rhs_scale=moving_scales, start=True, stop=True)
            return acc

        def gather(picked, window, h):
            V.tensor_copy(picked[:], window[:].indirect(offsets[:, h * JH // 16 : (h + 1) * JH // 16]))
            return picked

        col_words = [gather(sb.tile([P, JH], U16, name=f"col_words{h}", align_bytes=64), words, h) for h in both]
        col_scales = [gather(sb.tile([P, JH], U8, name="col_scales0", align_bytes=64), scales, 0)]
        w2_q = quantize("w2", weave("w2", w2_raw[:]))
        w1_q = quantize("w1", weave("w1", w1_raw[:]))
        col_scales.append(gather(sb.tile([P, JH], U8, name="col_scales1", tag="stage_b", align_bytes=64), scales, 1))
        a, b = [], []
        for h in both:
            b.append(product(f"b{h}", w2_q, col_words[h][:].bitcast(FP4X4), col_scales[h][:]))
            a.append(product(f"a{h}", w1_q, col_words[h][:].bitcast(FP4X4), col_scales[h][:]))

        last_raw = sb.tile([P, PACK * (R + G)], F32, name="last_raw")
        wo_raw = last_raw[:, 0 : PACK * R].rearrange("p (t c) -> p t c", t=PACK)
        dy_raw = last_raw[:, PACK * R :].rearrange("p (t c) -> p t c", t=PACK)
        nc.sync.dma_start(out=wo_raw, in_=by_rows(wo))
        nc.sync.dma_start(out=dy_raw, in_=by_rows(dy))
        tail_in = sb.tile([P, J + 8], F32, name="tail_in")
        base_sb = tail_in[:, 0:J]
        gain = tail_in[:, J : J + 1]
        nc.sync.dma_start(out=base_sb, in_=base)
        nc.sync.dma_start(out=gain, in_=og)

        def new(name, width):
            return [sb.tile([P, width], F32, name=f"{name}{h}") for h in both]

        p, pa, d, e, ee, pe, kp, t1, t2, t3, t4, y = [new(n, JH) for n in ("p", "pa", "d", "e", "ee", "pe", "kp", "t1", "t2", "t3", "t4", "y")]
        z, n1, m, u, ub, sa = [new(n, GH) for n in ("z", "n1", "m", "u", "ub", "sa")]
        cb = new("cb", 2 * GH)
        cbz = new("cbz", 2 * GH)
        rz_all, uu, nq, slope, kk = [sb.tile([P, G], F32, name=n) for n in ("rz_all", "uu", "nq", "slope", "kk")]
        rz = [rz_all[:, h * GH : (h + 1) * GH] for h in both]

        wo_woven = weave("wo", wo_raw)
        for h in both:
            nc.scalar.activation(out=p[h][:], in_=b[h][:], func=ACT.Exp)
        dy_woven = weave("dy", dy_raw)
        last_q = {}
        c0 = ps.tile([P, G], F32, name="c0")

        def s_z(h):
            V.tensor_reduce(out=z[h][:], in_=grouped(p[h][:]), axis=AX.X, op=ALU.add)

        def s_pa(h):
            V.tensor_tensor(pa[h][:], a[h][:], p[h][:], ALU.mult)

        def s_rz(h):
            V.reciprocal(rz[h], z[h][:])

        def s_n(h):
            V.tensor_reduce(out=n1[h][:], in_=grouped(pa[h][:]), axis=AX.X, op=ALU.add)

        def s_m(h):
            V.tensor_tensor(m[h][:], n1[h][:], rz[h], ALU.mult)
            nc.scalar.activation(out=u[h][:], in_=m[h][:], func=ACT.Tanh)
            nc.scalar.activation(out=uu[:, h * GH : (h + 1) * GH], in_=u[h][:], func=ACT.Square)

        def s_d(h):
            V.tensor_tensor(grouped(d[h][:]), grouped(a[h][:]), spread(m[h][:]), ALU.subtract)

        def s_e(h):
            V.tensor_tensor(e[h][:], d[h][:], p[h][:], ALU.mult)
            nc.scalar.activation(out=ee[h][:], in_=e[h][:], func=ACT.Square)

        def s_g(h):
            V.tensor_tensor(pe[h][:], e[h][:], p[h][:], ALU.mult)

        def s_wo(h):
            last_q["wo"] = quantize("wo", wo_woven)

        def s_dy(h):
            wo_q = last_q["wo"]
            dy_q = quantize("dy", dy_woven)
            nc.tensor.matmul_mx(out=c0[:], lhsT=wo_q[0][:].bitcast(FP8X4), lhsT_scale=wo_q[1][:],
                                rhs=dy_q[0][:].bitcast(FP8X4), rhs_scale=dy_q[1][:], start=True, stop=True)

        def s_nq(h):
            V.scalar_tensor_tensor(nq[:], uu[:], 1.0, c0[:], ALU.subtract, ALU.mult)

        def s_slope(h):
            V.tensor_tensor(slope[:], nq[:], rz_all[:], ALU.mult)
            nc.scalar.activation(out=kk[:], in_=slope[:], func=ACT.Square, scale=math.sqrt(2.0))

        def s_rf(h):
            V.tensor_reduce(out=cb[h][:, GH:], in_=grouped(ee[h][:]), axis=AX.X, op=ALU.add)

        def s_rg(h):
            V.tensor_reduce(out=sa[h][:], in_=grouped(pe[h][:]), axis=AX.X, op=ALU.add)

        def s_ub(h):
            V.scalar_tensor_tensor(ub[h][:], cb[h][:, GH:], 2.0, u[h][:], ALU.mult, ALU.mult)

        def s_cc(h):
            V.tensor_tensor(cb[h][:, 0:GH], sa[h][:], ub[h][:], ALU.add)

        def s_x(h):
            V.tensor_tensor(cbz[h][:].rearrange("p (s g) -> p s g", s=2), cb[h][:].rearrange("p (s g) -> p s g", s=2),
                            rz[h].rearrange("p (o g) -> p o g", o=1).to_broadcast([P, 2, GH]), ALU.mult)

        def s_kp(h):
            V.tensor_tensor(grouped(kp[h][:]), grouped(p[h][:]), spread(kk[:, h * GH : (h + 1) * GH]), ALU.mult)

        def s_t1(h):
            V.tensor_tensor(grouped(t1[h][:]), grouped(e[h][:]), spread(cbz[h][:, 0:GH]), ALU.subtract)

        def s_t2(h):
            V.tensor_tensor(t2[h][:], t1[h][:], d[h][:], ALU.mult)

        def s_t3(h):
            V.tensor_tensor(grouped(t3[h][:]), grouped(t2[h][:]), spread(cbz[h][:, GH:]), ALU.subtract)

        def s_t4(h):
            V.tensor_tensor(t4[h][:], t3[h][:], kp[h][:], ALU.mult)

        def s_y(h):
            pieces = [(0, JH)] if h == 0 else [(0, JH // 2), (JH // 2, JH)]
            for i, (lo, hi) in enumerate(pieces):
                V.scalar_tensor_tensor(y[h][:, lo:hi], t4[h][:, lo:hi], gain, base_sb[:, h * JH + lo : h * JH + hi], ALU.mult, ALU.add)
                queue = nc.scalar if len(pieces) - i == 2 else nc.sync
                queue.dma_start(out=out[:, h * JH + lo : h * JH + hi], in_=y[h][:, lo:hi])

        s_wo(0)
        s_z(0)
        s_pa(0)
        s_rz(0)
        s_n(0)
        s_z(1)
        s_m(0)
        s_pa(1)
        s_rz(1)
        s_d(0)
        s_n(1)
        s_e(0)
        s_m(1)
        s_dy(0)
        s_g(0)
        s_d(1)
        s_rg(0)
        s_e(1)
        s_rf(0)
        s_nq(0)
        s_g(1)
        s_slope(0)
        s_ub(0)
        s_rf(1)
        s_cc(0)
        s_rg(1)
        s_x(0)
        s_ub(1)
        s_kp(0)
        s_cc(1)
        s_t1(0)
        s_x(1)
        s_kp(1)
        s_t1(1)
        s_t2(0)
        s_t2(1)
        s_t3(0)
        s_t3(1)
        s_t4(0)
        s_t4(1)
        s_y(0)
        s_y(1)
